import numpy as np
import ml_dtypes


def mxq(x, axis, fmt="e4m3"):
    dtype, down = {"e4m3": (ml_dtypes.float8_e4m3fn, 7), "e5m2": (ml_dtypes.float8_e5m2, 14)}[fmt]
    v = np.moveaxis(np.asarray(x, np.float32).astype(ml_dtypes.bfloat16).astype(np.float64), axis, -1)
    blocks = v.reshape(v.shape[:-1] + (-1, 32))
    amax = np.abs(blocks).max(-1, keepdims=True)
    byte = np.maximum(np.where(amax > 0, np.frexp(amax)[1] - 1 + 127, 0) - down, 1)
    scale = np.exp2(byte - 127.0)
    codes = (blocks / scale).astype(np.float32).astype(dtype).astype(np.float64)
    return np.moveaxis((codes * scale).reshape(v.shape), -1, axis)


WIDE = False


def mx_kscale(k):
    if not WIDE:
        return np.ones(k)
    levels = np.array([10, -10, 5, -5, 0])
    if k % 512:
        return np.exp2(np.random.permutation(np.resize(levels, k // 32))).repeat(32)
    a = np.empty((k // 512, 16))
    for p in range(k // 512):
        a[p, :8] = np.random.permutation(np.resize(levels, 8))
        for g in range(8):
            far = levels[np.abs(levels - a[p, g]) >= 10]
            a[p, g + 8] = far[np.random.randint(len(far))]
    return np.exp2(a.ravel()).repeat(32)


def f64(x):
    return np.asarray(x).astype(np.float64)


def striped(idx):
    return np.tile(idx.reshape(-1, 16).T, (8, 1)).astype(np.uint16)


def unstriped(offs):
    return offs[:16].T.reshape(-1).astype(np.int64)


def pack_weight(w):
    k, n = w.shape
    w = f64(np.asarray(w, np.float32).astype(ml_dtypes.bfloat16)).reshape(k // 32, 32, n)
    amax = np.abs(w).max(1)
    byte = np.clip(np.where(amax > 0, np.frexp(amax)[1] - 1 + 127 - 7, 1), 1, 254)
    scaled = (w * np.exp2(127.0 - byte)[:, None, :]).reshape(k, n).astype(np.float32)
    words = np.ascontiguousarray(scaled.reshape(k // 512, 128, 4, n).transpose(0, 1, 3, 2)).astype(ml_dtypes.float8_e4m3fn).view(np.uint8)
    return words, np.ascontiguousarray(byte.astype(np.uint8).reshape(k // 512, 16, n))


def unpack_weight(words, scales):
    g, p, n, _ = words.shape
    vals = np.ascontiguousarray(words).view(ml_dtypes.float8_e4m3fn).astype(np.float64) * np.repeat(np.exp2(scales.astype(np.float64) - 127.0), 8, axis=1)[..., None]
    return vals.transpose(0, 1, 3, 2).reshape(g * 512, n)


K, T, S, N, H = 512, 2048, 512, 128, 512


def setup_inputs():
    n = np.random.standard_normal
    s = mx_kscale(K)[:, None]
    u = mx_kscale(H)
    packed_xT = pack_weight(n((K, T)) * s)
    return {
        "x_words": packed_xT[0],
        "x_scales": packed_xT[1],
        "w1": (n((K, H)) / np.sqrt(K) / s).astype(np.float32),
        "w2": (n((K, H)) / np.sqrt(K) / s).astype(np.float32),
        "unit": (np.random.uniform(0.6, 1.4, (H, 1)) * u[:, None]).astype(np.float32),
        "w3": (n((H, N)) / np.sqrt(H) / u[:, None]).astype(np.float32),
        "offs": striped(np.random.permutation(T)[:S]),
        "ea": striped(np.random.permutation(S)),
        "eb": striped(np.random.permutation(S)),
    }


def reference(x_words, x_scales, w1, w2, unit, w3, offs, ea, eb):
    xq = unpack_weight(x_words, x_scales)[:, unstriped(offs)]
    qs = mxq(f64(w1), 0, "e4m3").T @ xq
    qv = mxq(f64(w2), 0, "e4m3").T @ xq
    nrm = np.sqrt((qs) ** 2 + (qv) ** 2 + 0.1)
    us = qs / nrm
    sa = us[:, unstriped(ea)]
    sb = us[:, unstriped(eb)]
    ut = qv / nrm
    ta = ut[:, unstriped(ea)]
    tb = ut[:, unstriped(eb)]
    cs = sa * sb - (ta * tb)
    ct = sa * tb + ta * sb
    err = -1.0 * (cs * us + ct * ut) + 1.0
    wgt = np.exp(-1.2 * err)
    hid = f64(unit) * (wgt * (ct - ut))
    return mxq(f64(w3), 0, "e4m3").T @ mxq(hid, 0, "e4m3")

@@ -1,0 +1,197 @@
+from contextlib import ExitStack
+
+import concourse.mybir as mybir
+from concourse.masks import make_identity
+
+K, T, S, N, H = 512, 2048, 512, 128, 512
+FLOPS = 2 * K * H * S * 2 + 2 * H * N * S
+
+F32 = mybir.dt.float32
+BF16 = mybir.dt.bfloat16
+I32 = mybir.dt.int32
+U32 = mybir.dt.uint32
+U16 = mybir.dt.uint16
+U8 = mybir.dt.uint8
+FP8X4 = mybir.dt.float8_e4m3fn_x4
+ALU = mybir.AluOpType
+ACT = mybir.ActivationFunctionType
+
+P = 128
+PACK = 4
+TILES = H // P
+BLOCKS = S // P
+
+
+def tile_picked_ycycav_upd_p_kernel(tc, x_words, x_scales, w1, w2, unit, w3, offs, ea, eb, out):
+    nc = tc.nc
+    with ExitStack() as ctx:
+        keep = ctx.enter_context(tc.tile_pool(name="keep", bufs=1))
+        work = ctx.enter_context(tc.tile_pool(name="work", bufs=4))
+        psum = ctx.enter_context(tc.psum_pool(name="psum", bufs=8))
+
+        offs_t = keep.tile([P, S // 16], U16, name="offs_t")
+        ea_t = keep.tile([P, S // 16], U16, name="ea_t")
+        eb_t = keep.tile([P, S // 16], U16, name="eb_t")
+        xw = keep.tile([P, T], I32, name="xw", align_bytes=64)
+        xs = keep.tile([P, T], U8, name="xs", align_bytes=64)
+        ident = keep.tile([P, P], F32, name="ident", align_bytes=64)
+        unit_t = keep.tile([P, PACK], F32, name="unit_t")
+
+        def load_weight(w, cols, name):
+            raw = keep.tile([P, PACK, P], F32, name=name, align_bytes=64)
+            nc.sync.dma_start(out=raw[:], in_=w[:, cols].rearrange("(p j) c -> p j c", j=PACK))
+            return raw
+
+        xs_rows = keep.tile([P, T // 4], I32, name="xs_rows", align_bytes=64)
+        for q in range(4):
+            nc.sync.dma_start(out=xs_rows[32 * q : 32 * q + 4, :], in_=x_scales[0, 4 * q : 4 * q + 4, :].bitcast(I32))
+        nc.sync.dma_start(offs_t[:], offs)
+        nc.vector.memset(xs[:].bitcast(I32), 0)
+        for q in range(4):
+            nc.vector.tensor_copy(xs[32 * q : 32 * q + 4, :].bitcast(I32), xs_rows[32 * q : 32 * q + 4, :])
+        raws = []
+        raws.append((load_weight(w1, slice(0, P), "w1_0"), load_weight(w2, slice(0, P), "w2_0")))
+        nc.sync.dma_start(out=xw[:], in_=x_words[0].rearrange("p n t -> p (n t)").bitcast(I32))
+        for t in range(1, TILES):
+            cols = slice(t * P, (t + 1) * P)
+            raws.append((load_weight(w1, cols, "w1_%d" % t), load_weight(w2, cols, "w2_%d" % t)))
+            if t == 1:
+                nc.sync.dma_start(ea_t[:], ea)
+                nc.sync.dma_start(eb_t[:], eb)
+        w3_raw = load_weight(w3, slice(0, N), "w3_raw")
+        nc.sync.dma_start(out=unit_t[:], in_=unit.rearrange("(p t) o -> p (t o)", t=PACK))
+        make_identity(nc, ident[:])
+
+        def interleave(copy, grouped, raw):
+            copy(
+                out=grouped.rearrange("p (c i) j -> p c j i", i=4),
+                in_=raw.rearrange("p j (c i) -> p c j i", i=4),
+            )
+
+        def quantise(grouped, width, name):
+            codes = keep.tile([P, width], U32, name=name + "_codes", align_bytes=64)
+            scales = keep.tile([P, width], U8, name=name + "_scales", align_bytes=64)
+            nc.vector.quantize_mx(out=codes[:].bitcast(FP8X4), scales=scales[:], in_=grouped)
+            return codes, scales
+
+        def prepare_weights(t):
+            grouped = keep.tile([P, 2 * P, PACK], BF16, name="wg_%d" % t, align_bytes=64)
+            copy = nc.scalar.copy if t == 0 else nc.vector.tensor_copy
+            interleave(copy, grouped[:, 0:P, :], raws[t][0][:])
+            interleave(copy, grouped[:, P : 2 * P, :], raws[t][1][:])
+            return quantise(grouped[:].rearrange("p c j -> p (c j)"), 2 * P, "w_%d" % t)
+
+        wq = [prepare_weights(0)]
+        gs = keep.tile([P, S], U8, name="gs", align_bytes=64)
+        gw = keep.tile([P, S], U32, name="gw", align_bytes=64)
+        nc.vector.tensor_copy(gs[:], xs[:].indirect(offs_t[:]))
+        nc.vector.tensor_copy(gw[:], xw[:].bitcast(U32).indirect(offs_t[:]))
+
+        def normalise(t):
+            codes, scales = wq[t]
+            banks = []
+            sq = work.tile([P, 2, S], F32, name="sq")
+            for c in range(2):
+                bank = psum.tile([P, S], F32, name="q", tag="a")
+                cols = slice(c * P, (c + 1) * P)
+                nc.tensor.matmul_mx(
+                    out=bank[:], lhsT=codes[:, cols].bitcast(FP8X4), lhsT_scale=scales[:, cols],
+                    rhs=gw[:].bitcast(FP8X4), rhs_scale=gs[:], start=True, stop=True,
+                )
+                nc.scalar.activation(sq[:, c, :], bank[:], ACT.Square)
+                banks.append(bank)
+            n2 = work.tile([P, S], F32, name="n2")
+            nc.vector.scalar_tensor_tensor(n2[:], sq[:, 0, :], 0.1, sq[:, 1, :], ALU.add, ALU.add)
+            z = work.tile([P, 3 * S], F32, name="z")
+            nc.scalar.activation(z[:, 2 * S : 3 * S], n2[:], ACT.Abs_reciprocal_sqrt)
+            nc.vector.tensor_tensor(z[:, 0:S], banks[0][:], z[:, 2 * S : 3 * S], ALU.mult)
+            nc.vector.scalar_tensor_tensor(z[:, S : 2 * S], banks[1][:], -1.0, z[:, 2 * S : 3 * S], ALU.mult, ALU.mult)
+            return z
+
+        def fetch(z, j0, width, on_vector, tag):
+            g = keep.tile([P, 4, width], F32, name="g", tag=tag, align_bytes=64)
+            cols = slice(j0 // 16, (j0 + width) // 16)
+            for n, (lst, plane) in enumerate(((ea_t, 0), (ea_t, 1), (eb_t, 0), (eb_t, 1))):
+                window = z[:, plane * S : (plane + 2) * S].indirect(lst[:, cols])
+                if n in on_vector:
+                    nc.vector.tensor_copy(g[:, n, :], window)
+                else:
+                    nc.scalar.activation(g[:, n, :], window, ACT.Copy)
+            return g
+
+        def compose(z, g, j0, width, tag):
+            blocks = width // P
+            prod = work.tile([P, 4, width], F32, name="prod")
+            for b, a in ((0, 1), (0, 0), (1, 0), (1, 1)):
+                nc.vector.tensor_tensor(prod[:, 2 * b + a, :], g[:, a, :], g[:, 2 + b, :], ALU.mult)
+            c = work.tile([P, 2, width], F32, name="c", align_bytes=64)
+            nc.vector.scalar_tensor_tensor(c[:, 1, :], prod[:, 1, :], -1.0, prod[:, 2, :], ALU.mult, ALU.subtract)
+            nc.vector.tensor_tensor(c[:, 0, :], prod[:, 3, :], prod[:, 0, :], ALU.subtract)
+            m = keep.tile([P, 2, width], F32, name="m", tag=tag, align_bytes=64)
+            own = z[:, 0 : 2 * S].rearrange("p (a s) -> p a s", a=2)[:, :, j0 : j0 + width]
+            for a in (1, 0):
+                nc.vector.tensor_tensor(m[:, a, :], c[:, a, :], own[:, a, :], ALU.mult)
+            e_bank = psum.tile([P, blocks, P], F32, name="e_bank", tag="a")
+            d_bank = psum.tile([P, blocks, P], F32, name="d_bank", tag="a")
+            for jb in range(blocks):
+                cols = slice(jb * P, (jb + 1) * P)
+                nc.tensor.matmul(e_bank[:, jb, :], lhsT=own[:, 1, cols], rhs=ident[:], is_transpose=True, start=True, stop=False)
+                nc.tensor.matmul(e_bank[:, jb, :], lhsT=c[:, 1, cols], rhs=ident[:], is_transpose=True, start=False, stop=True)
+            for jb in range(blocks):
+                cols = slice(jb * P, (jb + 1) * P)
+                nc.tensor.matmul(d_bank[:, jb, :], lhsT=m[:, 1, cols], rhs=ident[:], is_transpose=True, start=True, stop=False)
+                nc.tensor.matmul(d_bank[:, jb, :], lhsT=m[:, 0, cols], rhs=ident[:], is_transpose=True, start=False, stop=True)
+            return e_bank, d_bank
+
+        def weigh(t, banks, j0, width):
+            e_bank, d_bank = banks
+            blocks = width // P
+            wgt = work.tile([P, blocks, PACK, P // PACK], F32, name="wgt")
+            nc.scalar.activation(wgt[:], d_bank[:].rearrange("p b (m s) -> p b s m", s=PACK), ACT.Exp, bias=-1.2, scale=-1.2)
+            nc.vector.tensor_tensor(
+                hid_t[:, j0 // P : j0 // P + blocks, :, 32 * t : 32 * (t + 1)],
+                e_bank[:].rearrange("p b (m s) -> p b s m", s=PACK), wgt[:], ALU.mult,
+            )
+
+        def finish(j0, width):
+            out_bank = psum.tile([P, width], F32, name="out_bank", tag="a")
+            for jb in range(j0 // P, (j0 + width) // P):
+                back = psum.tile([P, PACK, P], F32, name="back", tag="a")
+                for s in range(PACK):
+                    nc.tensor.transpose(back[:, s, :], hid_t[:, jb, s, :], ident[:])
+                hq = work.tile([P, P, PACK], BF16, name="hq", align_bytes=64)
+                nc.vector.tensor_tensor(
+                    hq[:], back[:].rearrange("p s j -> p j s"), unit_t[:].unsqueeze(1).to_broadcast([P, P, PACK]), ALU.mult,
+                )
+                codes, scales = quantise(hq[:].rearrange("p j s -> p (j s)"), P, "hid_%d" % jb)
+                nc.tensor.matmul_mx(
+                    out=out_bank[:, jb * P - j0 : (jb + 1) * P - j0], lhsT=w3_codes[:].bitcast(FP8X4), lhsT_scale=w3_scales[:],
+                    rhs=codes[:].bitcast(FP8X4), rhs_scale=scales[:], start=True, stop=True,
+                )
+            res = work.tile([P, width], F32, name="res")
+            nc.scalar.copy(res[:], out_bank[:])
+            nc.sync.dma_start(out=out[:, j0 : j0 + width], in_=res[:])
+
+        half = S // 2
+        zs = [normalise(0)]
+        g = fetch(zs[0], 0, S, (), "g0")
+        for t in range(1, TILES):
+            wq.append(prepare_weights(t))
+            zs.append(normalise(t))
+        w3_grouped = keep.tile([P, N, PACK], BF16, name="w3_grouped", align_bytes=64)
+        interleave(nc.vector.tensor_copy, w3_grouped[:], w3_raw[:])
+        w3_codes, w3_scales = quantise(w3_grouped[:].rearrange("p c j -> p (c j)"), N, "w3")
+        banks = [compose(zs[0], g, 0, S, "m0")]
+        for t in (1, 2):
+            banks.append(compose(zs[t], fetch(zs[t], 0, S, (), "g%d" % t), 0, S, "m%d" % t))
+        hid_t = keep.tile([P, BLOCKS, PACK, P], F32, name="hid_t", tag="g2", align_bytes=64)
+        weigh(0, banks[0], 0, S)
+        weigh(1, banks[1], 0, S)
+        first = compose(zs[3], fetch(zs[3], 0, half, (), "m1"), 0, half, "m3")
+        weigh(2, banks[2], 0, S)
+        g = fetch(zs[3], half, half, (), "m2")
+        weigh(3, first, 0, half)
+        second = compose(zs[3], g, half, half, "m4")
+        finish(0, half)
+        weigh(3, second, half, half)
+        finish(half, half)

@@ -26,172 +26,238 @@ def tile_picked_ycycav_upd_p_kernel(tc, x_words, x_scales, w1, w2, unit, w3, off
     nc = tc.nc
     with ExitStack() as ctx:
         keep = ctx.enter_context(tc.tile_pool(name="keep", bufs=1))
-        work = ctx.enter_context(tc.tile_pool(name="work", bufs=4))
-        psum = ctx.enter_context(tc.psum_pool(name="psum", bufs=8))
+        psum = ctx.enter_context(tc.psum_pool(name="psum", bufs=1))
 
+        def sbuf(name, shape, dtype):
+            return keep.tile(shape, dtype, name=name, align_bytes=64)
+
+        banks = [psum.tile([P, S], F32, name="bank%d" % b) for b in range(8)]
         offs_t = keep.tile([P, S // 16], U16, name="offs_t")
         ea_t = keep.tile([P, S // 16], U16, name="ea_t")
         eb_t = keep.tile([P, S // 16], U16, name="eb_t")
-        xw = keep.tile([P, T], I32, name="xw", align_bytes=64)
-        xs = keep.tile([P, T], U8, name="xs", align_bytes=64)
-        ident = keep.tile([P, P], F32, name="ident", align_bytes=64)
-        unit_t = keep.tile([P, PACK], F32, name="unit_t")
+        xw = sbuf("xw", [P, T], I32)
+        xs = sbuf("xs", [P, T], U8)
+        xs_rows = sbuf("xs_rows", [P, T // 4], I32)
+        ident = sbuf("ident", [P, P], F32)
+        unit_t = sbuf("unit_t", [P, PACK], F32)
 
         def load_weight(w, cols, name):
-            raw = keep.tile([P, PACK, P], F32, name=name, align_bytes=64)
+            raw = sbuf(name, [P, PACK, cols.stop - cols.start], F32)
             nc.sync.dma_start(out=raw[:], in_=w[:, cols].rearrange("(p j) c -> p j c", j=PACK))
             return raw
 
-        xs_rows = keep.tile([P, T // 4], I32, name="xs_rows", align_bytes=64)
         for q in range(4):
             nc.sync.dma_start(out=xs_rows[32 * q : 32 * q + 4, :], in_=x_scales[0, 4 * q : 4 * q + 4, :].bitcast(I32))
         nc.sync.dma_start(offs_t[:], offs)
+        raws = []
+        for first, count in ((0, 1), (1, 1), (2, 2)):
+            cols = slice(first * P, (first + count) * P)
+            pair = (load_weight(w1, cols, "w1_%d" % first), load_weight(w2, cols, "w2_%d" % first))
+            raws.extend([[raw[:, :, n * P : (n + 1) * P] for raw in pair] for n in range(count)])
+            if first == 0:
+                nc.sync.dma_start(out=xw[:], in_=x_words[0].rearrange("p n t -> p (n t)").bitcast(I32))
+            if first == 1:
+                nc.sync.dma_start(ea_t[:], ea)
+                nc.sync.dma_start(eb_t[:], eb)
+        w3_raw = load_weight(w3, slice(0, N), "w3_raw")[:]
+        nc.sync.dma_start(out=unit_t[:], in_=unit.rearrange("(p t) o -> p (t o)", t=PACK))
+        make_identity(nc, ident[:])
+        minus_unit = sbuf("minus_unit", [P, PACK], F32)
+        nc.gpsimd.tensor_scalar(minus_unit[:], unit_t[:], -1.0, 0.0, ALU.mult, ALU.add)
+        warm = sbuf("warm", [P, 1], F32)
+        nc.scalar.activation(warm[:], ident[:, 0:1], ACT.Abs_reciprocal_sqrt, bias=1.0)
+
+        half = S // 2
         nc.vector.memset(xs[:].bitcast(I32), 0)
         for q in range(4):
             nc.vector.tensor_copy(xs[32 * q : 32 * q + 4, :].bitcast(I32), xs_rows[32 * q : 32 * q + 4, :])
-        raws = []
-        raws.append((load_weight(w1, slice(0, P), "w1_0"), load_weight(w2, slice(0, P), "w2_0")))
-        nc.sync.dma_start(out=xw[:], in_=x_words[0].rearrange("p n t -> p (n t)").bitcast(I32))
-        for t in range(1, TILES):
-            cols = slice(t * P, (t + 1) * P)
-            raws.append((load_weight(w1, cols, "w1_%d" % t), load_weight(w2, cols, "w2_%d" % t)))
-            if t == 1:
-                nc.sync.dma_start(ea_t[:], ea)
-                nc.sync.dma_start(eb_t[:], eb)
-        w3_raw = load_weight(w3, slice(0, N), "w3_raw")
-        nc.sync.dma_start(out=unit_t[:], in_=unit.rearrange("(p t) o -> p (t o)", t=PACK))
-        make_identity(nc, ident[:])
-
-        def interleave(copy, grouped, raw):
-            copy(
-                out=grouped.rearrange("p (c i) j -> p c j i", i=4),
-                in_=raw.rearrange("p j (c i) -> p c j i", i=4),
-            )
+        gs = sbuf("gs", [P, S], U8)
+        gw = sbuf("gw", [P, S], U32)
+        nc.vector.tensor_copy(gs[:], xs[:].indirect(offs_t[:]))
+        for h in range(2):
+            nc.vector.tensor_copy(gw[:, h * half : (h + 1) * half], xw[:].bitcast(U32).indirect(offs_t[:, h * half // 16 : (h + 1) * half // 16]))
 
         def quantise(grouped, width, name):
-            codes = keep.tile([P, width], U32, name=name + "_codes", align_bytes=64)
-            scales = keep.tile([P, width], U8, name=name + "_scales", align_bytes=64)
+            codes = sbuf(name + "_codes", [P, width], U32)
+            scales = sbuf(name + "_scales", [P, width], U8)
             nc.vector.quantize_mx(out=codes[:].bitcast(FP8X4), scales=scales[:], in_=grouped)
             return codes, scales
 
-        def prepare_weights(t):
-            grouped = keep.tile([P, 2 * P, PACK], BF16, name="wg_%d" % t, align_bytes=64)
-            copy = nc.scalar.copy if t == 0 else nc.vector.tensor_copy
-            interleave(copy, grouped[:, 0:P, :], raws[t][0][:])
-            interleave(copy, grouped[:, P : 2 * P, :], raws[t][1][:])
-            return quantise(grouped[:].rearrange("p c j -> p (c j)"), 2 * P, "w_%d" % t)
-
-        wq = [prepare_weights(0)]
-        gs = keep.tile([P, S], U8, name="gs", align_bytes=64)
-        gw = keep.tile([P, S], U32, name="gw", align_bytes=64)
-        nc.vector.tensor_copy(gs[:], xs[:].indirect(offs_t[:]))
-        nc.vector.tensor_copy(gw[:], xw[:].bitcast(U32).indirect(offs_t[:]))
-
-        def normalise(t):
-            codes, scales = wq[t]
-            banks = []
-            sq = work.tile([P, 2, S], F32, name="sq")
-            for c in range(2):
-                bank = psum.tile([P, S], F32, name="q", tag="a")
-                cols = slice(c * P, (c + 1) * P)
-                nc.tensor.matmul_mx(
-                    out=bank[:], lhsT=codes[:, cols].bitcast(FP8X4), lhsT_scale=scales[:, cols],
-                    rhs=gw[:].bitcast(FP8X4), rhs_scale=gs[:], start=True, stop=True,
+        def prepare(raw_list, copies, name):
+            grouped = sbuf(name + "_bf16", [P, len(raw_list) * P, PACK], BF16)
+            for n, (raw, copy) in enumerate(zip(raw_list, copies)):
+                copy(
+                    out=grouped[:, n * P : (n + 1) * P, :].rearrange("p (c i) j -> p c j i", i=4),
+                    in_=raw.rearrange("p j (c i) -> p c j i", i=4),
                 )
-                nc.scalar.activation(sq[:, c, :], bank[:], ACT.Square)
-                banks.append(bank)
-            n2 = work.tile([P, S], F32, name="n2")
-            nc.vector.scalar_tensor_tensor(n2[:], sq[:, 0, :], 0.1, sq[:, 1, :], ALU.add, ALU.add)
-            z = work.tile([P, 3 * S], F32, name="z")
-            nc.scalar.activation(z[:, 2 * S : 3 * S], n2[:], ACT.Abs_reciprocal_sqrt)
-            nc.vector.tensor_tensor(z[:, 0:S], banks[0][:], z[:, 2 * S : 3 * S], ALU.mult)
-            nc.vector.scalar_tensor_tensor(z[:, S : 2 * S], banks[1][:], -1.0, z[:, 2 * S : 3 * S], ALU.mult, ALU.mult)
-            return z
+            codes, scales = quantise(grouped[:].rearrange("p c j -> p (c j)"), len(raw_list) * P, name)
+            return [(codes[:, n * P : (n + 1) * P], scales[:, n * P : (n + 1) * P]) for n in range(len(raw_list))]
 
-        def fetch(z, j0, width, on_vector, tag):
-            g = keep.tile([P, 4, width], F32, name="g", tag=tag, align_bytes=64)
+        zs = [sbuf("z%d" % t, [P, 3 * S], F32) for t in range(TILES)]
+        n2s = [sbuf("n2_%d" % t, [P, S], F32) for t in range(TILES)]
+        sqs = [sbuf("sq%d" % t, [P, 2 * S], F32) for t in range(TILES)]
+
+        def squares(t, weights):
+            for h in range(2):
+                for c, (codes, scales) in enumerate(weights):
+                    nc.tensor.matmul_mx(
+                        out=banks[2 * t + h][:, c * half : (c + 1) * half], lhsT=codes.bitcast(FP8X4), lhsT_scale=scales,
+                        rhs=gw[:, h * half : (h + 1) * half].bitcast(FP8X4), rhs_scale=gs[:, h * half : (h + 1) * half],
+                        start=True, stop=True,
+                    )
+                nc.scalar.activation(sqs[t][:, h * S : (h + 1) * S], banks[2 * t + h][:], ACT.Square)
+
+        def total(t, halves):
+            sq = sqs[t][:].rearrange("p (h c j) -> p h c j", h=2, c=2)
+            n2 = n2s[t][:].rearrange("p (h j) -> p h j", h=2)
+            for hs in halves:
+                nc.vector.scalar_tensor_tensor(n2[:, hs, :], sq[:, hs, 0, :], 0.1, sq[:, hs, 1, :], ALU.add, ALU.add)
+
+        def inverse(t, halves):
+            rinv = zs[t][:, 2 * S : 3 * S].rearrange("p (h j) -> p h j", h=2)
+            n2 = n2s[t][:].rearrange("p (h j) -> p h j", h=2)
+            for hs in halves:
+                nc.scalar.activation(rinv[:, hs, :], n2[:, hs, :], ACT.Abs_reciprocal_sqrt)
+
+        def scale(t):
+            z = zs[t][:].rearrange("p (a h j) -> p a h j", a=3, h=2)
+            for h in range(2):
+                nc.vector.tensor_tensor(
+                    z[:, 0:2, h, :], banks[2 * t + h][:].rearrange("p (c j) -> p c j", c=2),
+                    z[:, 2:3, h, :].to_broadcast([P, 2, half]), ALU.mult,
+                )
+
+        def fetch(z, j0, width, g, which=(0, 2, 1, 3), on_vector=()):
             cols = slice(j0 // 16, (j0 + width) // 16)
-            for n, (lst, plane) in enumerate(((ea_t, 0), (ea_t, 1), (eb_t, 0), (eb_t, 1))):
+            for n in which:
+                lst, plane = (ea_t, eb_t)[n // 2], n % 2
                 window = z[:, plane * S : (plane + 2) * S].indirect(lst[:, cols])
                 if n in on_vector:
-                    nc.vector.tensor_copy(g[:, n, :], window)
+                    nc.vector.tensor_copy(g[n], window)
                 else:
-                    nc.scalar.activation(g[:, n, :], window, ACT.Copy)
+                    nc.scalar.activation(g[n], window, ACT.Copy)
             return g
 
-        def compose(z, g, j0, width, tag):
-            blocks = width // P
-            prod = work.tile([P, 4, width], F32, name="prod")
-            for b, a in ((0, 1), (0, 0), (1, 0), (1, 1)):
-                nc.vector.tensor_tensor(prod[:, 2 * b + a, :], g[:, a, :], g[:, 2 + b, :], ALU.mult)
-            c = work.tile([P, 2, width], F32, name="c", align_bytes=64)
+        def products(g, prod):
+            for b, a in ((0, 0), (0, 1), (1, 0), (1, 1)):
+                nc.vector.tensor_tensor(prod[:, 2 * b + a, :], g[a], g[2 + b], ALU.mult)
+
+        def combine(z, j0, width, prod, c, m, e_bank, d_bank):
             nc.vector.scalar_tensor_tensor(c[:, 1, :], prod[:, 1, :], -1.0, prod[:, 2, :], ALU.mult, ALU.subtract)
             nc.vector.tensor_tensor(c[:, 0, :], prod[:, 3, :], prod[:, 0, :], ALU.subtract)
-            m = keep.tile([P, 2, width], F32, name="m", tag=tag, align_bytes=64)
-            own = z[:, 0 : 2 * S].rearrange("p (a s) -> p a s", a=2)[:, :, j0 : j0 + width]
+            own = z[:].rearrange("p (a s) -> p a s", a=3)[:, :, j0 : j0 + width]
             for a in (1, 0):
                 nc.vector.tensor_tensor(m[:, a, :], c[:, a, :], own[:, a, :], ALU.mult)
-            e_bank = psum.tile([P, blocks, P], F32, name="e_bank", tag="a")
-            d_bank = psum.tile([P, blocks, P], F32, name="d_bank", tag="a")
-            for jb in range(blocks):
-                cols = slice(jb * P, (jb + 1) * P)
-                nc.tensor.matmul(e_bank[:, jb, :], lhsT=own[:, 1, cols], rhs=ident[:], is_transpose=True, start=True, stop=False)
-                nc.tensor.matmul(e_bank[:, jb, :], lhsT=c[:, 1, cols], rhs=ident[:], is_transpose=True, start=False, stop=True)
-            for jb in range(blocks):
-                cols = slice(jb * P, (jb + 1) * P)
-                nc.tensor.matmul(d_bank[:, jb, :], lhsT=m[:, 1, cols], rhs=ident[:], is_transpose=True, start=True, stop=False)
-                nc.tensor.matmul(d_bank[:, jb, :], lhsT=m[:, 0, cols], rhs=ident[:], is_transpose=True, start=False, stop=True)
-            return e_bank, d_bank
+            for bank, first, second in ((e_bank, own[:, 1, :], c[:, 1, :]), (d_bank, m[:, 1, :], m[:, 0, :])):
+                for jb in range(width // P):
+                    cols = slice(jb * P, (jb + 1) * P)
+                    nc.tensor.matmul(bank[:, cols], lhsT=first[:, cols], rhs=ident[:], is_transpose=True, start=True, stop=False)
+                    nc.tensor.matmul(bank[:, cols], lhsT=second[:, cols], rhs=ident[:], is_transpose=True, start=False, stop=True)
 
-        def weigh(t, banks, j0, width):
-            e_bank, d_bank = banks
-            blocks = width // P
-            wgt = work.tile([P, blocks, PACK, P // PACK], F32, name="wgt")
-            nc.scalar.activation(wgt[:], d_bank[:].rearrange("p b (m s) -> p b s m", s=PACK), ACT.Exp, bias=-1.2, scale=-1.2)
-            nc.vector.tensor_tensor(
-                hid_t[:, j0 // P : j0 // P + blocks, :, 32 * t : 32 * (t + 1)],
-                e_bank[:].rearrange("p b (m s) -> p b s m", s=PACK), wgt[:], ALU.mult,
+        def dealt(bank):
+            return bank.rearrange("p (b m s) -> p b s m", m=P // PACK, s=PACK)
+
+        def weigh(t, j0, width, wgt, e_bank, d_bank):
+            wgt = wgt.rearrange("p (b s m) -> p b s m", s=PACK, m=P // PACK)
+            nc.scalar.activation(wgt, dealt(d_bank), ACT.Exp, bias=-1.2, scale=-1.2)
+            nc.vector.tensor_tensor(hid_t[:, j0 // P : (j0 + width) // P, :, 32 * t : 32 * (t + 1)], dealt(e_bank), wgt, ALU.mult)
+
+        def finish_block(jb, back, out_cols, on_scalar):
+            back = back.rearrange("p (s j) -> p s j", s=PACK)
+            for s in range(PACK):
+                nc.tensor.transpose(back[:, s, :], hid_t[:, jb, s, :], ident[:])
+            hq = sbuf("hq%d" % jb, [P, P, PACK], BF16)
+            if on_scalar:
+                planes = sbuf("planes%d" % jb, [P, PACK, P], BF16)
+                for s in range(PACK):
+                    nc.scalar.activation(planes[:, s, :], back[:, s, :], ACT.Copy, scale=minus_unit[:, s : s + 1])
+                nc.scalar.copy(
+                    out=hq[:].rearrange("p (c i) s -> p c s i", i=4), in_=planes[:].rearrange("p s (c i) -> p c s i", i=4)
+                )
+            else:
+                nc.vector.tensor_tensor(
+                    hq[:], back.rearrange("p s j -> p j s"), minus_unit[:].unsqueeze(1).to_broadcast([P, P, PACK]), ALU.mult,
+                )
+            codes, scales = quantise(hq[:].rearrange("p j s -> p (j s)"), P, "hid_%d" % jb)
+            nc.tensor.matmul_mx(
+                out=out_cols, lhsT=w3_codes.bitcast(FP8X4), lhsT_scale=w3_scales,
+                rhs=codes[:].bitcast(FP8X4), rhs_scale=scales[:], start=True, stop=True,
             )
 
-        def finish(j0, width):
-            out_bank = psum.tile([P, width], F32, name="out_bank", tag="a")
-            for jb in range(j0 // P, (j0 + width) // P):
-                back = psum.tile([P, PACK, P], F32, name="back", tag="a")
-                for s in range(PACK):
-                    nc.tensor.transpose(back[:, s, :], hid_t[:, jb, s, :], ident[:])
-                hq = work.tile([P, P, PACK], BF16, name="hq", align_bytes=64)
-                nc.vector.tensor_tensor(
-                    hq[:], back[:].rearrange("p s j -> p j s"), unit_t[:].unsqueeze(1).to_broadcast([P, P, PACK]), ALU.mult,
-                )
-                codes, scales = quantise(hq[:].rearrange("p j s -> p (j s)"), P, "hid_%d" % jb)
-                nc.tensor.matmul_mx(
-                    out=out_bank[:, jb * P - j0 : (jb + 1) * P - j0], lhsT=w3_codes[:].bitcast(FP8X4), lhsT_scale=w3_scales[:],
-                    rhs=codes[:].bitcast(FP8X4), rhs_scale=scales[:], start=True, stop=True,
-                )
-            res = work.tile([P, width], F32, name="res")
-            nc.scalar.copy(res[:], out_bank[:])
+        def store(j0, width, bank):
+            res = sbuf("res%d" % j0, [P, width], F32)
+            nc.scalar.copy(res[:], bank)
             nc.sync.dma_start(out=out[:, j0 : j0 + width], in_=res[:])
 
-        half = S // 2
-        zs = [normalise(0)]
-        g = fetch(zs[0], 0, S, (), "g0")
-        for t in range(1, TILES):
-            wq.append(prepare_weights(t))
-            zs.append(normalise(t))
-        w3_grouped = keep.tile([P, N, PACK], BF16, name="w3_grouped", align_bytes=64)
-        interleave(nc.vector.tensor_copy, w3_grouped[:], w3_raw[:])
-        w3_codes, w3_scales = quantise(w3_grouped[:].rearrange("p c j -> p (c j)"), N, "w3")
-        banks = [compose(zs[0], g, 0, S, "m0")]
-        for t in (1, 2):
-            banks.append(compose(zs[t], fetch(zs[t], 0, S, (), "g%d" % t), 0, S, "m%d" % t))
-        hid_t = keep.tile([P, BLOCKS, PACK, P], F32, name="hid_t", tag="g2", align_bytes=64)
-        weigh(0, banks[0], 0, S)
-        weigh(1, banks[1], 0, S)
-        first = compose(zs[3], fetch(zs[3], 0, half, (), "m1"), 0, half, "m3")
-        weigh(2, banks[2], 0, S)
-        g = fetch(zs[3], half, half, (), "m2")
-        weigh(3, first, 0, half)
-        second = compose(zs[3], g, half, half, "m4")
-        finish(0, half)
-        weigh(3, second, half, half)
-        finish(half, half)
+        def planes(name, n, width):
+            return sbuf(name, [P, n, width], F32)[:]
+
+        on_scalar, on_vector = nc.scalar.copy, nc.vector.tensor_copy
+        apart, whole = [slice(0, 1), slice(1, 2)], [slice(0, 2)]
+        prods = [planes("prod%d" % t, 4, S) for t in range(2)]
+        cs = [planes("c%d" % t, 2, S) for t in range(4)]
+        ms = [planes("m%d" % t, 2, S) for t in range(4)]
+        wgts = n2s[::-1]
+        g = [[sbuf("g%d_%d" % (t, n), [P, S], F32) for n in range(4)] for t in range(TILES)]
+        for t in range(TILES - 1):
+            g[t][1] = n2s[t + 1]
+        hid_t = sbuf("hid_t", [P, BLOCKS, PACK, P], F32)[:]
+
+        def sums(t, j0, width):
+            if width == S:
+                return banks[2 * t][:], banks[2 * t + 1][:]
+            bank = banks[2 * t + j0 // half]
+            return bank[:, 0:width], bank[:, width : 2 * width]
+
+        def fetch_piece(t, j0, width, on_vector=()):
+            fetch(zs[t], j0, width, [plane[:, j0 : j0 + width] for plane in g[t]], on_vector=on_vector)
+
+        def products_piece(t, j0, width):
+            products([plane[:, j0 : j0 + width] for plane in g[t]], prods[t % 2][:, :, j0 : j0 + width])
+
+        def combine_piece(t, j0, width):
+            cols = slice(j0, j0 + width)
+            combine(zs[t], j0, width, prods[t % 2][:, :, cols], cs[t][:, :, cols], ms[t][:, :, cols], *sums(t, j0, width))
+
+        def weigh_piece(t, j0, width):
+            weigh(t, j0, width, wgts[t][:, j0 : j0 + width], *sums(t, j0, width))
+
+        squares(0, prepare(raws[0], [on_scalar, on_scalar], "w_0"))
+        total(0, apart)
+        inverse(0, apart)
+        squares(1, prepare(raws[1], [on_vector, on_vector], "w_1"))
+        scale(0)
+        total(1, whole)
+        inverse(1, whole)
+        fetch_piece(0, 0, S, on_vector=(2,))
+        squares(2, prepare(raws[2], [on_vector, on_vector], "w_2"))
+        weights = prepare(raws[3], [on_vector, on_vector], "w_3")
+        ((w3_codes, w3_scales),) = prepare([w3_raw], [on_vector], "w3")
+        for t in (0, 1):
+            scale(t + 1)
+            products_piece(t, 0, S)
+            total(t + 2, whole)
+            inverse(t + 2, whole)
+            if t == 0:
+                squares(3, weights)
+            fetch_piece(t + 1, 0, S)
+            combine_piece(t, 0, S)
+        scale(3)
+        fetch_piece(3, 0, half)
+        fetch_piece(3, half, half)
+        products_piece(2, 0, S)
+        combine_piece(2, 0, S)
+        products_piece(3, 0, half)
+        combine_piece(3, 0, half)
+        for t in range(3):
+            weigh_piece(t, 0, S)
+        weigh_piece(3, 0, half)
+        products_piece(3, half, half)
+        combine_piece(3, half, half)
+        weigh_piece(3, half, half)
+        finish_block(0, banks[0][:], banks[4][:, 0:P], True)
+        finish_block(1, banks[1][:], banks[4][:, P : 2 * P], False)
+        store(0, half, banks[4][:, 0:half])
+        finish_block(2, banks[2][:], banks[5][:, 0:P], False)
+        finish_block(3, banks[3][:], banks[5][:, P : 2 * P], False)
+        store(half, half, banks[5][:, 0:half])

@@ -20,6 +20,12 @@ P = 128
 PACK = 4
 TILES = H // P
 BLOCKS = S // P
+HALF = S // 2
+LAST = TILES - 1
+LIST_ROWS = 16
+QUADRANT = 32
+HALVES = (slice(0, HALF), slice(HALF, S))
+WHOLE = slice(0, S)
 
 
 def tile_picked_ycycav_upd_p_kernel(tc, x_words, x_scales, w1, w2, unit, w3, offs, ea, eb, out):
@@ -31,233 +37,219 @@ def tile_picked_ycycav_upd_p_kernel(tc, x_words, x_scales, w1, w2, unit, w3, off
         def sbuf(name, shape, dtype):
             return keep.tile(shape, dtype, name=name, align_bytes=64)
 
-        banks = [psum.tile([P, S], F32, name="bank%d" % b) for b in range(8)]
-        offs_t = keep.tile([P, S // 16], U16, name="offs_t")
-        ea_t = keep.tile([P, S // 16], U16, name="ea_t")
-        eb_t = keep.tile([P, S // 16], U16, name="eb_t")
-        xw = sbuf("xw", [P, T], I32)
-        xs = sbuf("xs", [P, T], U8)
-        xs_rows = sbuf("xs_rows", [P, T // 4], I32)
-        ident = sbuf("ident", [P, P], F32)
-        unit_t = sbuf("unit_t", [P, PACK], F32)
+        def per_tile(name, shape):
+            return [sbuf("%s%d" % (name, t), shape, F32) for t in range(TILES)]
 
-        def load_weight(w, cols, name):
+        banks = [psum.tile([P, S], F32, name="bank%d" % b) for b in range(2 * TILES)]
+
+        def load_list(name, source):
+            tile = keep.tile([P, S // LIST_ROWS], U16, name=name)
+            nc.sync.dma_start(tile[:], source)
+            return tile
+
+        def load_weight(name, w, cols):
             raw = sbuf(name, [P, PACK, cols.stop - cols.start], F32)
-            nc.sync.dma_start(out=raw[:], in_=w[:, cols].rearrange("(p j) c -> p j c", j=PACK))
+            nc.sync.dma_start(out=raw[:], in_=w[:, cols].rearrange("(p s) c -> p s c", s=PACK))
             return raw
 
-        for q in range(4):
-            nc.sync.dma_start(out=xs_rows[32 * q : 32 * q + 4, :], in_=x_scales[0, 4 * q : 4 * q + 4, :].bitcast(I32))
-        nc.sync.dma_start(offs_t[:], offs)
-        raws = []
-        for first, count in ((0, 1), (1, 1), (2, 2)):
-            cols = slice(first * P, (first + count) * P)
-            pair = (load_weight(w1, cols, "w1_%d" % first), load_weight(w2, cols, "w2_%d" % first))
-            raws.extend([[raw[:, :, n * P : (n + 1) * P] for raw in pair] for n in range(count)])
-            if first == 0:
-                nc.sync.dma_start(out=xw[:], in_=x_words[0].rearrange("p n t -> p (n t)").bitcast(I32))
-            if first == 1:
-                nc.sync.dma_start(ea_t[:], ea)
-                nc.sync.dma_start(eb_t[:], eb)
-        w3_raw = load_weight(w3, slice(0, N), "w3_raw")[:]
-        nc.sync.dma_start(out=unit_t[:], in_=unit.rearrange("(p t) o -> p (t o)", t=PACK))
+        w1_first = load_weight("w1_0", w1, slice(0, P))
+        scale_rows = sbuf("scale_rows", [P, T // 4], I32)
+        quadrants = [slice(QUADRANT * q, QUADRANT * q + 4) for q in range(P // QUADRANT)]
+        for q, rows in enumerate(quadrants):
+            nc.sync.dma_start(out=scale_rows[rows, :], in_=x_scales[0, 4 * q : 4 * q + 4, :].bitcast(I32))
+        offs_t = load_list("offs_t", offs)
+        raws = [[w1_first[:], load_weight("w2_0", w2, slice(0, P))[:]]]
+        words = sbuf("words", [P, T], I32)
+        nc.sync.dma_start(out=words[:], in_=x_words[0].rearrange("p n s -> p (n s)").bitcast(I32))
+        raws.append([load_weight("w1_1", w1, slice(P, 2 * P))[:], load_weight("w2_1", w2, slice(P, 2 * P))[:]])
+        lists = (load_list("ea_t", ea), load_list("eb_t", eb))
+        rest = (load_weight("w1_rest", w1, slice(2 * P, H)), load_weight("w2_rest", w2, slice(2 * P, H)))
+        raws.extend([[raw[:, :, n * P : (n + 1) * P] for raw in rest] for n in range(TILES - 2)])
+        w3_raw = load_weight("w3_raw", w3, slice(0, N))
+        unit_t = sbuf("unit_t", [P, PACK], F32)
+        nc.sync.dma_start(out=unit_t[:], in_=unit.rearrange("(p s) o -> p (s o)", s=PACK))
+
+        ident = sbuf("ident", [P, P], F32)
         make_identity(nc, ident[:])
-        minus_unit = sbuf("minus_unit", [P, PACK], F32)
-        nc.gpsimd.tensor_scalar(minus_unit[:], unit_t[:], -1.0, 0.0, ALU.mult, ALU.add)
         warm = sbuf("warm", [P, 1], F32)
         nc.scalar.activation(warm[:], ident[:, 0:1], ACT.Abs_reciprocal_sqrt, bias=1.0)
 
-        half = S // 2
-        nc.vector.memset(xs[:].bitcast(I32), 0)
-        for q in range(4):
-            nc.vector.tensor_copy(xs[32 * q : 32 * q + 4, :].bitcast(I32), xs_rows[32 * q : 32 * q + 4, :])
-        gs = sbuf("gs", [P, S], U8)
-        gw = sbuf("gw", [P, S], U32)
-        nc.vector.tensor_copy(gs[:], xs[:].indirect(offs_t[:]))
-        for h in range(2):
-            nc.vector.tensor_copy(gw[:, h * half : (h + 1) * half], xw[:].bitcast(U32).indirect(offs_t[:, h * half // 16 : (h + 1) * half // 16]))
+        scale_bytes = sbuf("scale_bytes", [P, T], U8)
+        nc.vector.memset(scale_bytes[:].bitcast(I32), 0)
+        for rows in quadrants:
+            nc.vector.tensor_copy(scale_bytes[rows, :].bitcast(I32), scale_rows[rows, :])
+        x_plane = sbuf("x_plane", [P, S], U8)
+        x_codes = sbuf("x_codes", [P, S], U32)
 
-        def quantise(grouped, width, name):
+        def entries(lst, cols):
+            return lst[:, cols.start // LIST_ROWS : cols.stop // LIST_ROWS]
+
+        nc.vector.tensor_copy(x_plane[:], scale_bytes[:].indirect(offs_t[:]))
+        for cols in HALVES:
+            nc.vector.tensor_copy(x_codes[:, cols], words[:].bitcast(U32).indirect(entries(offs_t, cols)))
+
+        def quantise(name, grouped):
+            width = grouped.shape[1]
             codes = sbuf(name + "_codes", [P, width], U32)
-            scales = sbuf(name + "_scales", [P, width], U8)
-            nc.vector.quantize_mx(out=codes[:].bitcast(FP8X4), scales=scales[:], in_=grouped)
-            return codes, scales
+            plane = sbuf(name + "_plane", [P, width], U8)
+            nc.vector.quantize_mx(out=codes[:].bitcast(FP8X4), scales=plane[:], in_=grouped.rearrange("p c s -> p (c s)"))
+            return codes, plane
 
-        def prepare(raw_list, copies, name):
+        def quantise_weights(name, raw_list, copy):
             grouped = sbuf(name + "_bf16", [P, len(raw_list) * P, PACK], BF16)
-            for n, (raw, copy) in enumerate(zip(raw_list, copies)):
+            spans = [slice(n * P, (n + 1) * P) for n in range(len(raw_list))]
+            for raw, span in zip(raw_list, spans):
                 copy(
-                    out=grouped[:, n * P : (n + 1) * P, :].rearrange("p (c i) j -> p c j i", i=4),
-                    in_=raw.rearrange("p j (c i) -> p c j i", i=4),
+                    out=grouped[:, span, :].rearrange("p (c i) s -> p c s i", i=4),
+                    in_=raw.rearrange("p s (c i) -> p c s i", i=4),
                 )
-            codes, scales = quantise(grouped[:].rearrange("p c j -> p (c j)"), len(raw_list) * P, name)
-            return [(codes[:, n * P : (n + 1) * P], scales[:, n * P : (n + 1) * P]) for n in range(len(raw_list))]
+            codes, plane = quantise(name, grouped[:])
+            return [(codes[:, span], plane[:, span]) for span in spans]
 
-        zs = [sbuf("z%d" % t, [P, 3 * S], F32) for t in range(TILES)]
-        n2s = [sbuf("n2_%d" % t, [P, S], F32) for t in range(TILES)]
-        sqs = [sbuf("sq%d" % t, [P, 2 * S], F32) for t in range(TILES)]
+        z = per_tile("z", [P, 3, S])
+        squares = per_tile("squares", [P, 2, 2, HALF])
+        norms = per_tile("norms", [P, S])
 
-        def squares(t, weights):
-            for h in range(2):
-                for c, (codes, scales) in enumerate(weights):
+        def project(t, weights):
+            for h, cols in enumerate(HALVES):
+                bank = banks[2 * t + h]
+                for (codes, plane), side in zip(weights, HALVES):
                     nc.tensor.matmul_mx(
-                        out=banks[2 * t + h][:, c * half : (c + 1) * half], lhsT=codes.bitcast(FP8X4), lhsT_scale=scales,
-                        rhs=gw[:, h * half : (h + 1) * half].bitcast(FP8X4), rhs_scale=gs[:, h * half : (h + 1) * half],
-                        start=True, stop=True,
+                        out=bank[:, side], lhsT=codes.bitcast(FP8X4), lhsT_scale=plane,
+                        rhs=x_codes[:, cols].bitcast(FP8X4), rhs_scale=x_plane[:, cols], start=True, stop=True,
                     )
-                nc.scalar.activation(sqs[t][:, h * S : (h + 1) * S], banks[2 * t + h][:], ACT.Square)
+                nc.scalar.activation(squares[t][:, h].rearrange("p c j -> p (c j)"), bank[:], ACT.Square)
 
-        def total(t, halves):
-            sq = sqs[t][:].rearrange("p (h c j) -> p h c j", h=2, c=2)
-            n2 = n2s[t][:].rearrange("p (h j) -> p h j", h=2)
-            for hs in halves:
-                nc.vector.scalar_tensor_tensor(n2[:, hs, :], sq[:, hs, 0, :], 0.1, sq[:, hs, 1, :], ALU.add, ALU.add)
+        def invert(t, halves):
+            cols = slice(halves.start * HALF, halves.stop * HALF)
+            nc.vector.scalar_tensor_tensor(
+                norms[t][:, cols].rearrange("p (h j) -> p h j", j=HALF),
+                squares[t][:, halves, 0, :], 0.1, squares[t][:, halves, 1, :], ALU.add, ALU.add,
+            )
+            nc.scalar.activation(z[t][:, 2, cols], norms[t][:, cols], ACT.Abs_reciprocal_sqrt)
 
-        def inverse(t, halves):
-            rinv = zs[t][:, 2 * S : 3 * S].rearrange("p (h j) -> p h j", h=2)
-            n2 = n2s[t][:].rearrange("p (h j) -> p h j", h=2)
-            for hs in halves:
-                nc.scalar.activation(rinv[:, hs, :], n2[:, hs, :], ACT.Abs_reciprocal_sqrt)
-
-        def scale(t):
-            z = zs[t][:].rearrange("p (a h j) -> p a h j", a=3, h=2)
-            for h in range(2):
+        def normalise(t):
+            for h, cols in enumerate(HALVES):
                 nc.vector.tensor_tensor(
-                    z[:, 0:2, h, :], banks[2 * t + h][:].rearrange("p (c j) -> p c j", c=2),
-                    z[:, 2:3, h, :].to_broadcast([P, 2, half]), ALU.mult,
+                    z[t][:, 0:2, cols], banks[2 * t + h][:].rearrange("p (c j) -> p c j", c=2),
+                    z[t][:, 2:3, cols].to_broadcast([P, 2, HALF]), ALU.mult,
                 )
 
-        def fetch(z, j0, width, g, which=(0, 2, 1, 3), on_vector=()):
-            cols = slice(j0 // 16, (j0 + width) // 16)
-            for n in which:
-                lst, plane = (ea_t, eb_t)[n // 2], n % 2
-                window = z[:, plane * S : (plane + 2) * S].indirect(lst[:, cols])
+        SA, TA, SB, TB = range(4)
+        fetched = []
+        for t in range(TILES):
+            own = sbuf("fetched%d" % t, [P, 4 if t == LAST else 2, S], F32)
+            if t == LAST:
+                fetched.append([own[:, n, :] for n in range(4)])
+            else:
+                fetched.append([own[:, 0, :], norms[t + 1][:], own[:, 1, :], squares[t + 1][:, 0].rearrange("p c j -> p (c j)")])
+
+        def fetch(t, cols, on_vector=()):
+            flat = z[t][:].rearrange("p a j -> p (a j)")
+            for n in (SA, SB, TA, TB):
+                first = (n % 2) * S
+                window = flat[:, first : first + 2 * S].indirect(entries(lists[n // 2], cols))
                 if n in on_vector:
-                    nc.vector.tensor_copy(g[n], window)
+                    nc.vector.tensor_copy(fetched[t][n][:, cols], window)
                 else:
-                    nc.scalar.activation(g[n], window, ACT.Copy)
-            return g
+                    nc.scalar.activation(fetched[t][n][:, cols], window, ACT.Copy)
 
-        def products(g, prod):
-            for b, a in ((0, 0), (0, 1), (1, 0), (1, 1)):
-                nc.vector.tensor_tensor(prod[:, 2 * b + a, :], g[a], g[2 + b], ALU.mult)
+        prods = [sbuf("prods%d" % n, [P, 4, S], F32) for n in range(2)]
+        minus_c = per_tile("minus_c", [P, 2, S])
+        terms = per_tile("terms", [P, 2, S])
+        wgts = norms[::-1]
 
-        def combine(z, j0, width, prod, c, m, e_bank, d_bank):
+        def sums(t, cols):
+            if t == LAST and cols.start:
+                return banks[1][:, HALVES[0]], banks[1][:, HALVES[1]]
+            return banks[2 * t][:, cols], banks[2 * t + 1][:, cols]
+
+        def multiply(t, cols):
+            for n, (a, b) in enumerate(((SA, SB), (TA, SB), (SA, TB), (TA, TB))):
+                nc.vector.tensor_tensor(prods[t % 2][:, n, cols], fetched[t][a][:, cols], fetched[t][b][:, cols], ALU.mult)
+
+        def combine(t, cols):
+            prod, c, m = prods[t % 2][:, :, cols], minus_c[t][:, :, cols], terms[t][:, :, cols]
             nc.vector.scalar_tensor_tensor(c[:, 1, :], prod[:, 1, :], -1.0, prod[:, 2, :], ALU.mult, ALU.subtract)
             nc.vector.tensor_tensor(c[:, 0, :], prod[:, 3, :], prod[:, 0, :], ALU.subtract)
-            own = z[:].rearrange("p (a s) -> p a s", a=3)[:, :, j0 : j0 + width]
-            for a in (1, 0):
-                nc.vector.tensor_tensor(m[:, a, :], c[:, a, :], own[:, a, :], ALU.mult)
-            for bank, first, second in ((e_bank, own[:, 1, :], c[:, 1, :]), (d_bank, m[:, 1, :], m[:, 0, :])):
-                for jb in range(width // P):
-                    cols = slice(jb * P, (jb + 1) * P)
-                    nc.tensor.matmul(bank[:, cols], lhsT=first[:, cols], rhs=ident[:], is_transpose=True, start=True, stop=False)
-                    nc.tensor.matmul(bank[:, cols], lhsT=second[:, cols], rhs=ident[:], is_transpose=True, start=False, stop=True)
+            for n in (1, 0):
+                nc.vector.tensor_tensor(m[:, n, :], c[:, n, :], z[t][:, n, cols], ALU.mult)
+            for total, first, second in zip(sums(t, cols), (z[t][:, 1, cols], m[:, 1, :]), (c[:, 1, :], m[:, 0, :])):
+                for j0 in range(0, cols.stop - cols.start, P):
+                    block = slice(j0, j0 + P)
+                    nc.tensor.matmul(total[:, block], lhsT=first[:, block], rhs=ident[:], is_transpose=True, start=True, stop=False)
+                    nc.tensor.matmul(total[:, block], lhsT=second[:, block], rhs=ident[:], is_transpose=True, start=False, stop=True)
 
-        def dealt(bank):
-            return bank.rearrange("p (b m s) -> p b s m", m=P // PACK, s=PACK)
+        rows_per_plane = P // PACK
 
-        def weigh(t, j0, width, wgt, e_bank, d_bank):
-            wgt = wgt.rearrange("p (b s m) -> p b s m", s=PACK, m=P // PACK)
-            nc.scalar.activation(wgt, dealt(d_bank), ACT.Exp, bias=-1.2, scale=-1.2)
-            nc.vector.tensor_tensor(hid_t[:, j0 // P : (j0 + width) // P, :, 32 * t : 32 * (t + 1)], dealt(e_bank), wgt, ALU.mult)
+        def dealt(turned):
+            return turned.rearrange("p (b m s) -> p b s m", m=rows_per_plane, s=PACK)
 
-        def finish_block(jb, back, out_cols, on_scalar):
-            back = back.rearrange("p (s j) -> p s j", s=PACK)
-            for s in range(PACK):
-                nc.tensor.transpose(back[:, s, :], hid_t[:, jb, s, :], ident[:])
-            hq = sbuf("hq%d" % jb, [P, P, PACK], BF16)
-            if on_scalar:
-                planes = sbuf("planes%d" % jb, [P, PACK, P], BF16)
-                for s in range(PACK):
-                    nc.scalar.activation(planes[:, s, :], back[:, s, :], ACT.Copy, scale=minus_unit[:, s : s + 1])
-                nc.scalar.copy(
-                    out=hq[:].rearrange("p (c i) s -> p c s i", i=4), in_=planes[:].rearrange("p s (c i) -> p c s i", i=4)
-                )
-            else:
-                nc.vector.tensor_tensor(
-                    hq[:], back.rearrange("p s j -> p j s"), minus_unit[:].unsqueeze(1).to_broadcast([P, P, PACK]), ALU.mult,
-                )
-            codes, scales = quantise(hq[:].rearrange("p j s -> p (j s)"), P, "hid_%d" % jb)
-            nc.tensor.matmul_mx(
-                out=out_cols, lhsT=w3_codes.bitcast(FP8X4), lhsT_scale=w3_scales,
-                rhs=codes[:].bitcast(FP8X4), rhs_scale=scales[:], start=True, stop=True,
+        def wgt_view(t, cols):
+            return wgts[t][:, cols].rearrange("p (b s m) -> p b s m", s=PACK, m=rows_per_plane)
+
+        def exponentiate(t, cols):
+            nc.scalar.activation(wgt_view(t, cols), dealt(sums(t, cols)[1]), ACT.Exp, bias=-1.2, scale=-1.2)
+
+        turned = sbuf("turned", [P, BLOCKS, PACK, P], F32)
+
+        def weigh(t, cols):
+            nc.vector.tensor_tensor(
+                turned[:, cols.start // P : cols.stop // P, :, rows_per_plane * t : rows_per_plane * (t + 1)],
+                dealt(sums(t, cols)[0]), wgt_view(t, cols), ALU.mult,
             )
 
-        def store(j0, width, bank):
-            res = sbuf("res%d" % j0, [P, width], F32)
-            nc.scalar.copy(res[:], bank)
-            nc.sync.dma_start(out=out[:, j0 : j0 + width], in_=res[:])
+        def finish(b, back_bank, result):
+            back = back_bank[:].rearrange("p (s j) -> p s j", s=PACK)
+            for s in range(PACK):
+                nc.tensor.transpose(back[:, s, :], turned[:, b, s, :], ident[:])
+            hid = sbuf("hid%d" % b, [P, P, PACK], BF16)
+            nc.vector.scalar_tensor_tensor(
+                hid[:], back.rearrange("p s j -> p j s"), -1.0,
+                unit_t[:].unsqueeze(1).to_broadcast([P, P, PACK]), ALU.mult, ALU.mult,
+            )
+            codes, plane = quantise("hid%d" % b, hid[:])
+            nc.tensor.matmul_mx(
+                out=result, lhsT=w3_codes.bitcast(FP8X4), lhsT_scale=w3_plane,
+                rhs=codes[:].bitcast(FP8X4), rhs_scale=plane[:], start=True, stop=True,
+            )
 
-        def planes(name, n, width):
-            return sbuf(name, [P, n, width], F32)[:]
-
-        on_scalar, on_vector = nc.scalar.copy, nc.vector.tensor_copy
-        apart, whole = [slice(0, 1), slice(1, 2)], [slice(0, 2)]
-        prods = [planes("prod%d" % t, 4, S) for t in range(2)]
-        cs = [planes("c%d" % t, 2, S) for t in range(4)]
-        ms = [planes("m%d" % t, 2, S) for t in range(4)]
-        wgts = n2s[::-1]
-        g = [[sbuf("g%d_%d" % (t, n), [P, S], F32) for n in range(4)] for t in range(TILES)]
-        for t in range(TILES - 1):
-            g[t][1] = n2s[t + 1]
-        hid_t = sbuf("hid_t", [P, BLOCKS, PACK, P], F32)[:]
-
-        def sums(t, j0, width):
-            if width == S:
-                return banks[2 * t][:], banks[2 * t + 1][:]
-            bank = banks[2 * t + j0 // half]
-            return bank[:, 0:width], bank[:, width : 2 * width]
-
-        def fetch_piece(t, j0, width, on_vector=()):
-            fetch(zs[t], j0, width, [plane[:, j0 : j0 + width] for plane in g[t]], on_vector=on_vector)
-
-        def products_piece(t, j0, width):
-            products([plane[:, j0 : j0 + width] for plane in g[t]], prods[t % 2][:, :, j0 : j0 + width])
-
-        def combine_piece(t, j0, width):
-            cols = slice(j0, j0 + width)
-            combine(zs[t], j0, width, prods[t % 2][:, :, cols], cs[t][:, :, cols], ms[t][:, :, cols], *sums(t, j0, width))
-
-        def weigh_piece(t, j0, width):
-            weigh(t, j0, width, wgts[t][:, j0 : j0 + width], *sums(t, j0, width))
-
-        squares(0, prepare(raws[0], [on_scalar, on_scalar], "w_0"))
-        total(0, apart)
-        inverse(0, apart)
-        squares(1, prepare(raws[1], [on_vector, on_vector], "w_1"))
-        scale(0)
-        total(1, whole)
-        inverse(1, whole)
-        fetch_piece(0, 0, S, on_vector=(2,))
-        squares(2, prepare(raws[2], [on_vector, on_vector], "w_2"))
-        weights = prepare(raws[3], [on_vector, on_vector], "w_3")
-        ((w3_codes, w3_scales),) = prepare([w3_raw], [on_vector], "w3")
-        for t in (0, 1):
-            scale(t + 1)
-            products_piece(t, 0, S)
-            total(t + 2, whole)
-            inverse(t + 2, whole)
-            if t == 0:
-                squares(3, weights)
-            fetch_piece(t + 1, 0, S)
-            combine_piece(t, 0, S)
-        scale(3)
-        fetch_piece(3, 0, half)
-        fetch_piece(3, half, half)
-        products_piece(2, 0, S)
-        combine_piece(2, 0, S)
-        products_piece(3, 0, half)
-        combine_piece(3, 0, half)
-        for t in range(3):
-            weigh_piece(t, 0, S)
-        weigh_piece(3, 0, half)
-        products_piece(3, half, half)
-        combine_piece(3, half, half)
-        weigh_piece(3, half, half)
-        finish_block(0, banks[0][:], banks[4][:, 0:P], True)
-        finish_block(1, banks[1][:], banks[4][:, P : 2 * P], False)
-        store(0, half, banks[4][:, 0:half])
-        finish_block(2, banks[2][:], banks[5][:, 0:P], False)
-        finish_block(3, banks[3][:], banks[5][:, P : 2 * P], False)
-        store(half, half, banks[5][:, 0:half])
+        project(0, quantise_weights("w_0", raws[0], nc.scalar.copy))
+        invert(0, slice(0, 1))
+        invert(0, slice(1, 2))
+        project(1, quantise_weights("w_1", raws[1], nc.vector.tensor_copy))
+        normalise(0)
+        invert(1, slice(0, 2))
+        fetch(0, WHOLE, on_vector=(SB,))
+        project(2, quantise_weights("w_2", raws[2], nc.vector.tensor_copy))
+        last_weights = quantise_weights("w_3", raws[LAST], nc.vector.tensor_copy)
+        ((w3_codes, w3_plane),) = quantise_weights("w3", [w3_raw[:]], nc.vector.tensor_copy)
+        normalise(1)
+        project(LAST, last_weights)
+        for t in range(TILES - 2):
+            multiply(t, WHOLE)
+            invert(t + 2, slice(0, 2))
+            fetch(t + 1, WHOLE)
+            combine(t, WHOLE)
+            normalise(t + 2)
+        for cols in HALVES:
+            fetch(LAST, cols)
+        multiply(LAST - 1, WHOLE)
+        combine(LAST - 1, WHOLE)
+        multiply(LAST, HALVES[0])
+        combine(LAST, HALVES[0])
+        for t in range(LAST):
+            exponentiate(t, WHOLE)
+        multiply(LAST, HALVES[1])
+        combine(LAST, HALVES[1])
+        for cols in HALVES:
+            exponentiate(LAST, cols)
+            for t in range(TILES):
+                weigh(t, cols)
+        back_banks = [banks[n] for n in (3, 5, 7, 6)]
+        for cols, bank in zip(HALVES, (banks[0], banks[2])):
+            for b in range(cols.start // P, cols.stop // P):
+                finish(b, back_banks[b], bank[:, b * P : (b + 1) * P])
+            result = sbuf("result%d" % cols.start, [P, HALF], F32)
+            nc.scalar.copy(result[:], bank[:, cols])
+            nc.sync.dma_start(out=out[:, cols], in_=result[:])

@@ -64,7 +64,6 @@ def tile_picked_ycycav_upd_p_kernel(tc, x_words, x_scales, w1, w2, unit, w3, off
         raws.append([load_weight("w1_1", w1, slice(P, 2 * P))[:], load_weight("w2_1", w2, slice(P, 2 * P))[:]])
         lists = (load_list("ea_t", ea), load_list("eb_t", eb))
         rest = (load_weight("w1_rest", w1, slice(2 * P, H)), load_weight("w2_rest", w2, slice(2 * P, H)))
-        raws.extend([[raw[:, :, n * P : (n + 1) * P] for raw in rest] for n in range(TILES - 2)])
         w3_raw = load_weight("w3_raw", w3, slice(0, N))
         unit_t = sbuf("unit_t", [P, PACK], F32)
         nc.sync.dma_start(out=unit_t[:], in_=unit.rearrange("(p s) o -> p (s o)", s=PACK))
@@ -142,7 +141,7 @@ def tile_picked_ycycav_upd_p_kernel(tc, x_words, x_scales, w1, w2, unit, w3, off
             if t == LAST:
                 fetched.append([own[:, n, :] for n in range(4)])
             else:
-                fetched.append([own[:, 0, :], norms[t + 1][:], own[:, 1, :], squares[t + 1][:, 0].rearrange("p c j -> p (c j)")])
+                fetched.append([own[:, 0, :], squares[t + 1][:, 0].rearrange("p c j -> p (c j)"), own[:, 1, :], norms[t + 1][:]])
 
         def fetch(t, cols, on_vector=()):
             flat = z[t][:].rearrange("p a j -> p (a j)")
@@ -157,7 +156,7 @@ def tile_picked_ycycav_upd_p_kernel(tc, x_words, x_scales, w1, w2, unit, w3, off
         prods = [sbuf("prods%d" % n, [P, 4, S], F32) for n in range(2)]
         minus_c = per_tile("minus_c", [P, 2, S])
         terms = per_tile("terms", [P, 2, S])
-        wgts = norms[::-1]
+        wgts = [fetched[2][TB], fetched[2][TA], norms[1][:], norms[0][:]]
 
         def sums(t, cols):
             if t == LAST and cols.start:
@@ -174,7 +173,7 @@ def tile_picked_ycycav_upd_p_kernel(tc, x_words, x_scales, w1, w2, unit, w3, off
             nc.vector.tensor_tensor(c[:, 0, :], prod[:, 3, :], prod[:, 0, :], ALU.subtract)
             for n in (1, 0):
                 nc.vector.tensor_tensor(m[:, n, :], c[:, n, :], z[t][:, n, cols], ALU.mult)
-            for total, first, second in zip(sums(t, cols), (z[t][:, 1, cols], m[:, 1, :]), (c[:, 1, :], m[:, 0, :])):
+            for total, first, second in zip(sums(t, cols), (c[:, 1, :], m[:, 1, :]), (z[t][:, 1, cols], m[:, 0, :])):
                 for j0 in range(0, cols.stop - cols.start, P):
                     block = slice(j0, j0 + P)
                     nc.tensor.matmul(total[:, block], lhsT=first[:, block], rhs=ident[:], is_transpose=True, start=True, stop=False)
@@ -199,20 +198,29 @@ def tile_picked_ycycav_upd_p_kernel(tc, x_words, x_scales, w1, w2, unit, w3, off
                 dealt(sums(t, cols)[0]), wgt_view(t, cols), ALU.mult,
             )
 
-        def finish(b, back_bank, result):
-            back = back_bank[:].rearrange("p (s j) -> p s j", s=PACK)
+        hid = sbuf("hid", [P, S, PACK], BF16)
+
+        def turn_back(b, bank):
             for s in range(PACK):
-                nc.tensor.transpose(back[:, s, :], turned[:, b, s, :], ident[:])
-            hid = sbuf("hid%d" % b, [P, P, PACK], BF16)
+                nc.tensor.transpose(bank[:, s * P : (s + 1) * P], turned[:, b, s, :], ident[:])
+
+        def round_hid(b, bank):
             nc.vector.scalar_tensor_tensor(
-                hid[:], back.rearrange("p s j -> p j s"), -1.0,
+                hid[:, b * P : (b + 1) * P, :], bank[:].rearrange("p (s j) -> p j s", s=PACK), -1.0,
                 unit_t[:].unsqueeze(1).to_broadcast([P, P, PACK]), ALU.mult, ALU.mult,
             )
-            codes, plane = quantise("hid%d" % b, hid[:])
+
+        def view(cols, bank):
+            codes, plane = quantise("hid%d" % cols.start, hid[:, cols, :])
             nc.tensor.matmul_mx(
-                out=result, lhsT=w3_codes.bitcast(FP8X4), lhsT_scale=w3_plane,
+                out=bank[:, cols], lhsT=w3_codes.bitcast(FP8X4), lhsT_scale=w3_plane,
                 rhs=codes[:].bitcast(FP8X4), rhs_scale=plane[:], start=True, stop=True,
             )
+
+        def store(cols, bank):
+            result = sbuf("result%d" % cols.start, [P, cols.stop - cols.start], F32)
+            nc.scalar.copy(result[:], bank[:, cols])
+            nc.sync.dma_start(out=out[:, cols], in_=result[:])
 
         project(0, quantise_weights("w_0", raws[0], nc.scalar.copy))
         invert(0, slice(0, 1))
@@ -221,8 +229,18 @@ def tile_picked_ycycav_upd_p_kernel(tc, x_words, x_scales, w1, w2, unit, w3, off
         normalise(0)
         invert(1, slice(0, 2))
         fetch(0, WHOLE, on_vector=(SB,))
-        project(2, quantise_weights("w_2", raws[2], nc.vector.tensor_copy))
-        last_weights = quantise_weights("w_3", raws[LAST], nc.vector.tensor_copy)
+        late = sbuf("late_bf16", [P, 2, 2, P, PACK], BF16)
+        for n, raw in enumerate(rest):
+            nc.vector.tensor_copy(
+                out=late[:, :, n].rearrange("p t (c i) s -> p t c s i", i=4),
+                in_=raw[:].rearrange("p s (t c i) -> p t c s i", t=2, i=4),
+            )
+        late_weights = []
+        for n in range(2):
+            codes, plane = quantise("late%d" % n, late[:, n].rearrange("p m c s -> p (m c) s"))
+            late_weights.append([(codes[:, span], plane[:, span]) for span in (slice(0, P), slice(P, 2 * P))])
+        project(2, late_weights[0])
+        last_weights = late_weights[1]
         ((w3_codes, w3_plane),) = quantise_weights("w3", [w3_raw[:]], nc.vector.tensor_copy)
         normalise(1)
         project(LAST, last_weights)
@@ -247,9 +265,12 @@ def tile_picked_ycycav_upd_p_kernel(tc, x_words, x_scales, w1, w2, unit, w3, off
             for t in range(TILES):
                 weigh(t, cols)
         back_banks = [banks[n] for n in (3, 5, 7, 6)]
-        for cols, bank in zip(HALVES, (banks[0], banks[2])):
-            for b in range(cols.start // P, cols.stop // P):
-                finish(b, back_banks[b], bank[:, b * P : (b + 1) * P])
-            result = sbuf("result%d" % cols.start, [P, HALF], F32)
-            nc.scalar.copy(result[:], bank[:, cols])
-            nc.sync.dma_start(out=out[:, cols], in_=result[:])
+        for b in range(BLOCKS):
+            turn_back(b, back_banks[b])
+        for b in range(BLOCKS):
+            round_hid(b, back_banks[b])
+        view(HALVES[0], banks[0])
+        store(HALVES[0], banks[0])
+        for b in (2, 3):
+            view(slice(b * P, (b + 1) * P), banks[2])
+        store(HALVES[1], banks[2])

@@ -24,6 +24,8 @@ HALF = S // 2
 LAST = TILES - 1
 LIST_ROWS = 16
 QUADRANT = 32
+SCALE_ROWS = 4
+RUN = 4
 HALVES = (slice(0, HALF), slice(HALF, S))
 WHOLE = slice(0, S)
 
@@ -54,9 +56,10 @@ def tile_picked_ycycav_upd_p_kernel(tc, x_words, x_scales, w1, w2, unit, w3, off
 
         w1_first = load_weight("w1_0", w1, slice(0, P))
         scale_rows = sbuf("scale_rows", [P, T // 4], I32)
-        quadrants = [slice(QUADRANT * q, QUADRANT * q + 4) for q in range(P // QUADRANT)]
+        quadrants = [slice(QUADRANT * q, QUADRANT * q + SCALE_ROWS) for q in range(P // QUADRANT)]
         for q, rows in enumerate(quadrants):
-            nc.sync.dma_start(out=scale_rows[rows, :], in_=x_scales[0, 4 * q : 4 * q + 4, :].bitcast(I32))
+            source = x_scales[0, SCALE_ROWS * q : SCALE_ROWS * (q + 1), :]
+            nc.sync.dma_start(out=scale_rows[rows, :], in_=source.bitcast(I32))
         offs_t = load_list("offs_t", offs)
         raws = [[w1_first[:], load_weight("w2_0", w2, slice(0, P))[:]]]
         words = sbuf("words", [P, T], I32)
@@ -99,14 +102,16 @@ def tile_picked_ycycav_upd_p_kernel(tc, x_words, x_scales, w1, w2, unit, w3, off
             spans = [slice(n * P, (n + 1) * P) for n in range(len(raw_list))]
             for raw, span in zip(raw_list, spans):
                 copy(
-                    out=grouped[:, span, :].rearrange("p (c i) s -> p c s i", i=4),
-                    in_=raw.rearrange("p s (c i) -> p c s i", i=4),
+                    out=grouped[:, span, :].rearrange("p (c i) s -> p c s i", i=RUN),
+                    in_=raw.rearrange("p s (c i) -> p c s i", i=RUN),
                 )
             codes, plane = quantise(name, grouped[:])
             return [(codes[:, span], plane[:, span]) for span in spans]
 
         z = per_tile("z", [P, 3, S])
-        squares = per_tile("squares", [P, 2, 2, HALF])
+        minus_c = per_tile("minus_c", [P, 2, S])
+        squares = [sbuf("squares%d" % t, [P, 2, 2, HALF], F32)[:] for t in range(LAST)]
+        squares.append(minus_c[0][:].rearrange("p h (c j) -> p h c j", c=2))
         norms = per_tile("norms", [P, S])
 
         def project(t, weights):
@@ -154,9 +159,8 @@ def tile_picked_ycycav_upd_p_kernel(tc, x_words, x_scales, w1, w2, unit, w3, off
                     nc.scalar.activation(fetched[t][n][:, cols], window, ACT.Copy)
 
         prods = [sbuf("prods%d" % n, [P, 4, S], F32) for n in range(2)]
-        minus_c = per_tile("minus_c", [P, 2, S])
         terms = per_tile("terms", [P, 2, S])
-        wgts = [fetched[2][TB], fetched[2][TA], norms[1][:], norms[0][:]]
+        wgts = [fetched[LAST - 1][TB], fetched[LAST - 1][TA], norms[1][:], norms[0][:]]
 
         def sums(t, cols):
             if t == LAST and cols.start:
@@ -179,13 +183,13 @@ def tile_picked_ycycav_upd_p_kernel(tc, x_words, x_scales, w1, w2, unit, w3, off
                     nc.tensor.matmul(total[:, block], lhsT=first[:, block], rhs=ident[:], is_transpose=True, start=True, stop=False)
                     nc.tensor.matmul(total[:, block], lhsT=second[:, block], rhs=ident[:], is_transpose=True, start=False, stop=True)
 
-        rows_per_plane = P // PACK
+        rows_per_slab = P // PACK
 
-        def dealt(turned):
-            return turned.rearrange("p (b m s) -> p b s m", m=rows_per_plane, s=PACK)
+        def dealt(total):
+            return total.rearrange("p (b m s) -> p b s m", m=rows_per_slab, s=PACK)
 
         def wgt_view(t, cols):
-            return wgts[t][:, cols].rearrange("p (b s m) -> p b s m", s=PACK, m=rows_per_plane)
+            return wgts[t][:, cols].rearrange("p (b s m) -> p b s m", s=PACK, m=rows_per_slab)
 
         def exponentiate(t, cols):
             nc.scalar.activation(wgt_view(t, cols), dealt(sums(t, cols)[1]), ACT.Exp, bias=-1.2, scale=-1.2)
@@ -194,7 +198,7 @@ def tile_picked_ycycav_upd_p_kernel(tc, x_words, x_scales, w1, w2, unit, w3, off
 
         def weigh(t, cols):
             nc.vector.tensor_tensor(
-                turned[:, cols.start // P : cols.stop // P, :, rows_per_plane * t : rows_per_plane * (t + 1)],
+                turned[:, cols.start // P : cols.stop // P, :, rows_per_slab * t : rows_per_slab * (t + 1)],
                 dealt(sums(t, cols)[0]), wgt_view(t, cols), ALU.mult,
             )
 
@@ -210,7 +214,7 @@ def tile_picked_ycycav_upd_p_kernel(tc, x_words, x_scales, w1, w2, unit, w3, off
                 unit_t[:].unsqueeze(1).to_broadcast([P, P, PACK]), ALU.mult, ALU.mult,
             )
 
-        def view(cols, bank):
+        def last_product(cols, bank):
             codes, plane = quantise("hid%d" % cols.start, hid[:, cols, :])
             nc.tensor.matmul_mx(
                 out=bank[:, cols], lhsT=w3_codes.bitcast(FP8X4), lhsT_scale=w3_plane,
@@ -232,23 +236,23 @@ def tile_picked_ycycav_upd_p_kernel(tc, x_words, x_scales, w1, w2, unit, w3, off
         late = sbuf("late_bf16", [P, 2, 2, P, PACK], BF16)
         for n, raw in enumerate(rest):
             nc.vector.tensor_copy(
-                out=late[:, :, n].rearrange("p t (c i) s -> p t c s i", i=4),
-                in_=raw[:].rearrange("p s (t c i) -> p t c s i", t=2, i=4),
+                out=late[:, :, n].rearrange("p t (c i) s -> p t c s i", i=RUN),
+                in_=raw[:].rearrange("p s (t c i) -> p t c s i", t=2, i=RUN),
             )
         late_weights = []
         for n in range(2):
             codes, plane = quantise("late%d" % n, late[:, n].rearrange("p m c s -> p (m c) s"))
             late_weights.append([(codes[:, span], plane[:, span]) for span in (slice(0, P), slice(P, 2 * P))])
         project(2, late_weights[0])
-        last_weights = late_weights[1]
         ((w3_codes, w3_plane),) = quantise_weights("w3", [w3_raw[:]], nc.vector.tensor_copy)
         normalise(1)
-        project(LAST, last_weights)
         for t in range(TILES - 2):
             multiply(t, WHOLE)
             invert(t + 2, slice(0, 2))
             fetch(t + 1, WHOLE)
             combine(t, WHOLE)
+            if t == 0:
+                project(LAST, late_weights[1])
             normalise(t + 2)
         for cols in HALVES:
             fetch(LAST, cols)
@@ -269,8 +273,8 @@ def tile_picked_ycycav_upd_p_kernel(tc, x_words, x_scales, w1, w2, unit, w3, off
             turn_back(b, back_banks[b])
         for b in range(BLOCKS):
             round_hid(b, back_banks[b])
-        view(HALVES[0], banks[0])
+        last_product(HALVES[0], banks[0])
         store(HALVES[0], banks[0])
-        for b in (2, 3):
-            view(slice(b * P, (b + 1) * P), banks[2])
+        for b in range(HALF // P, BLOCKS):
+            last_product(slice(b * P, (b + 1) * P), banks[2])
         store(HALVES[1], banks[2])

from contextlib import ExitStack

import concourse.mybir as mybir
from concourse.masks import make_identity

K, T, S, N, H = 512, 2048, 512, 128, 512
FLOPS = 2 * K * H * S * 2 + 2 * H * N * S

F32 = mybir.dt.float32
BF16 = mybir.dt.bfloat16
I32 = mybir.dt.int32
U32 = mybir.dt.uint32
U16 = mybir.dt.uint16
U8 = mybir.dt.uint8
FP8X4 = mybir.dt.float8_e4m3fn_x4
ALU = mybir.AluOpType
ACT = mybir.ActivationFunctionType

P = 128
PACK = 4
TILES = H // P
BLOCKS = S // P
HALF = S // 2
LAST = TILES - 1
LIST_ROWS = 16
QUADRANT = 32
SCALE_ROWS = 4
RUN = 4
HALVES = (slice(0, HALF), slice(HALF, S))
WHOLE = slice(0, S)


def tile_picked_ycycav_upd_p_kernel(tc, x_words, x_scales, w1, w2, unit, w3, offs, ea, eb, out):
    nc = tc.nc
    with ExitStack() as ctx:
        keep = ctx.enter_context(tc.tile_pool(name="keep", bufs=1))
        psum = ctx.enter_context(tc.psum_pool(name="psum", bufs=1))

        def sbuf(name, shape, dtype):
            return keep.tile(shape, dtype, name=name, align_bytes=64)

        def per_tile(name, shape):
            return [sbuf("%s%d" % (name, t), shape, F32) for t in range(TILES)]

        banks = [psum.tile([P, S], F32, name="bank%d" % b) for b in range(2 * TILES)]

        def load_list(name, source):
            tile = keep.tile([P, S // LIST_ROWS], U16, name=name)
            nc.sync.dma_start(tile[:], source)
            return tile

        def load_weight(name, w, cols):
            raw = sbuf(name, [P, PACK, cols.stop - cols.start], F32)
            nc.sync.dma_start(out=raw[:], in_=w[:, cols].rearrange("(p s) c -> p s c", s=PACK))
            return raw

        w1_first = load_weight("w1_0", w1, slice(0, P))
        scale_rows = sbuf("scale_rows", [P, T // 4], I32)
        quadrants = [slice(QUADRANT * q, QUADRANT * q + SCALE_ROWS) for q in range(P // QUADRANT)]
        for q, rows in enumerate(quadrants):
            source = x_scales[0, SCALE_ROWS * q : SCALE_ROWS * (q + 1), :]
            nc.sync.dma_start(out=scale_rows[rows, :], in_=source.bitcast(I32))
        offs_t = load_list("offs_t", offs)
        raws = [[w1_first[:], load_weight("w2_0", w2, slice(0, P))[:]]]
        words = sbuf("words", [P, T], I32)
        nc.sync.dma_start(out=words[:], in_=x_words[0].rearrange("p n s -> p (n s)").bitcast(I32))
        raws.append([load_weight("w1_1", w1, slice(P, 2 * P))[:], load_weight("w2_1", w2, slice(P, 2 * P))[:]])
        lists = (load_list("ea_t", ea), load_list("eb_t", eb))
        rest = (load_weight("w1_rest", w1, slice(2 * P, H)), load_weight("w2_rest", w2, slice(2 * P, H)))
        w3_raw = load_weight("w3_raw", w3, slice(0, N))
        unit_t = sbuf("unit_t", [P, PACK], F32)
        nc.sync.dma_start(out=unit_t[:], in_=unit.rearrange("(p s) o -> p (s o)", s=PACK))

        ident = sbuf("ident", [P, P], F32)
        make_identity(nc, ident[:])
        warm = sbuf("warm", [P, 1], F32)
        nc.scalar.activation(warm[:], ident[:, 0:1], ACT.Abs_reciprocal_sqrt, bias=1.0)

        scale_bytes = sbuf("scale_bytes", [P, T], U8)
        nc.vector.memset(scale_bytes[:].bitcast(I32), 0)
        for rows in quadrants:
            nc.vector.tensor_copy(scale_bytes[rows, :].bitcast(I32), scale_rows[rows, :])
        x_plane = sbuf("x_plane", [P, S], U8)
        x_codes = sbuf("x_codes", [P, S], U32)

        def entries(lst, cols):
            return lst[:, cols.start // LIST_ROWS : cols.stop // LIST_ROWS]

        nc.vector.tensor_copy(x_plane[:], scale_bytes[:].indirect(offs_t[:]))
        for cols in HALVES:
            nc.vector.tensor_copy(x_codes[:, cols], words[:].bitcast(U32).indirect(entries(offs_t, cols)))

        def quantise(name, grouped):
            width = grouped.shape[1]
            codes = sbuf(name + "_codes", [P, width], U32)
            plane = sbuf(name + "_plane", [P, width], U8)
            nc.vector.quantize_mx(out=codes[:].bitcast(FP8X4), scales=plane[:], in_=grouped.rearrange("p c s -> p (c s)"))
            return codes, plane

        def quantise_weights(name, raw_list, copy):
            grouped = sbuf(name + "_bf16", [P, len(raw_list) * P, PACK], BF16)
            spans = [slice(n * P, (n + 1) * P) for n in range(len(raw_list))]
            for raw, span in zip(raw_list, spans):
                copy(
                    out=grouped[:, span, :].rearrange("p (c i) s -> p c s i", i=RUN),
                    in_=raw.rearrange("p s (c i) -> p c s i", i=RUN),
                )
            codes, plane = quantise(name, grouped[:])
            return [(codes[:, span], plane[:, span]) for span in spans]

        z = per_tile("z", [P, 3, S])
        minus_c = per_tile("minus_c", [P, 2, S])
        squares = [sbuf("squares%d" % t, [P, 2, 2, HALF], F32)[:] for t in range(LAST)]
        squares.append(minus_c[0][:].rearrange("p h (c j) -> p h c j", c=2))
        norms = per_tile("norms", [P, S])

        def project(t, weights):
            for h, cols in enumerate(HALVES):
                bank = banks[2 * t + h]
                for (codes, plane), side in zip(weights, HALVES):
                    nc.tensor.matmul_mx(
                        out=bank[:, side], lhsT=codes.bitcast(FP8X4), lhsT_scale=plane,
                        rhs=x_codes[:, cols].bitcast(FP8X4), rhs_scale=x_plane[:, cols], start=True, stop=True,
                    )
                nc.scalar.activation(squares[t][:, h].rearrange("p c j -> p (c j)"), bank[:], ACT.Square)

        def invert(t, halves):
            cols = slice(halves.start * HALF, halves.stop * HALF)
            nc.vector.scalar_tensor_tensor(
                norms[t][:, cols].rearrange("p (h j) -> p h j", j=HALF),
                squares[t][:, halves, 0, :], 0.1, squares[t][:, halves, 1, :], ALU.add, ALU.add,
            )
            nc.scalar.activation(z[t][:, 2, cols], norms[t][:, cols], ACT.Abs_reciprocal_sqrt)

        def normalise(t):
            for h, cols in enumerate(HALVES):
                nc.vector.tensor_tensor(
                    z[t][:, 0:2, cols], banks[2 * t + h][:].rearrange("p (c j) -> p c j", c=2),
                    z[t][:, 2:3, cols].to_broadcast([P, 2, HALF]), ALU.mult,
                )

        SA, TA, SB, TB = range(4)
        fetched = []
        for t in range(TILES):
            own = sbuf("fetched%d" % t, [P, 4 if t == LAST else 2, S], F32)
            if t == LAST:
                fetched.append([own[:, n, :] for n in range(4)])
            else:
                fetched.append([own[:, 0, :], squares[t + 1][:, 0].rearrange("p c j -> p (c j)"), own[:, 1, :], norms[t + 1][:]])

        def fetch(t, cols, on_vector=()):
            flat = z[t][:].rearrange("p a j -> p (a j)")
            for n in (SA, SB, TA, TB):
                first = (n % 2) * S
                window = flat[:, first : first + 2 * S].indirect(entries(lists[n // 2], cols))
                if n in on_vector:
                    nc.vector.tensor_copy(fetched[t][n][:, cols], window)
                else:
                    nc.scalar.activation(fetched[t][n][:, cols], window, ACT.Copy)

        prods = [sbuf("prods%d" % n, [P, 4, S], F32) for n in range(2)]
        terms = per_tile("terms", [P, 2, S])
        wgts = [fetched[LAST - 1][TB], fetched[LAST - 1][TA], norms[1][:], norms[0][:]]

        def sums(t, cols):
            if t == LAST and cols.start:
                return banks[1][:, HALVES[0]], banks[1][:, HALVES[1]]
            return banks[2 * t][:, cols], banks[2 * t + 1][:, cols]

        def multiply(t, cols):
            for n, (a, b) in enumerate(((SA, SB), (TA, SB), (SA, TB), (TA, TB))):
                nc.vector.tensor_tensor(prods[t % 2][:, n, cols], fetched[t][a][:, cols], fetched[t][b][:, cols], ALU.mult)

        def combine(t, cols):
            prod, c, m = prods[t % 2][:, :, cols], minus_c[t][:, :, cols], terms[t][:, :, cols]
            nc.vector.scalar_tensor_tensor(c[:, 1, :], prod[:, 1, :], -1.0, prod[:, 2, :], ALU.mult, ALU.subtract)
            nc.vector.tensor_tensor(c[:, 0, :], prod[:, 3, :], prod[:, 0, :], ALU.subtract)
            for n in (1, 0):
                nc.vector.tensor_tensor(m[:, n, :], c[:, n, :], z[t][:, n, cols], ALU.mult)
            for total, first, second in zip(sums(t, cols), (c[:, 1, :], m[:, 1, :]), (z[t][:, 1, cols], m[:, 0, :])):
                for j0 in range(0, cols.stop - cols.start, P):
                    block = slice(j0, j0 + P)
                    nc.tensor.matmul(total[:, block], lhsT=first[:, block], rhs=ident[:], is_transpose=True, start=True, stop=False)
                    nc.tensor.matmul(total[:, block], lhsT=second[:, block], rhs=ident[:], is_transpose=True, start=False, stop=True)

        rows_per_slab = P // PACK

        def dealt(total):
            return total.rearrange("p (b m s) -> p b s m", m=rows_per_slab, s=PACK)

        def wgt_view(t, cols):
            return wgts[t][:, cols].rearrange("p (b s m) -> p b s m", s=PACK, m=rows_per_slab)

        def exponentiate(t, cols):
            nc.scalar.activation(wgt_view(t, cols), dealt(sums(t, cols)[1]), ACT.Exp, bias=-1.2, scale=-1.2)

        turned = sbuf("turned", [P, BLOCKS, PACK, P], F32)

        def weigh(t, cols):
            nc.vector.tensor_tensor(
                turned[:, cols.start // P : cols.stop // P, :, rows_per_slab * t : rows_per_slab * (t + 1)],
                dealt(sums(t, cols)[0]), wgt_view(t, cols), ALU.mult,
            )

        hid = sbuf("hid", [P, S, PACK], BF16)

        def turn_back(b, bank):
            for s in range(PACK):
                nc.tensor.transpose(bank[:, s * P : (s + 1) * P], turned[:, b, s, :], ident[:])

        def round_hid(b, bank):
            nc.vector.scalar_tensor_tensor(
                hid[:, b * P : (b + 1) * P, :], bank[:].rearrange("p (s j) -> p j s", s=PACK), -1.0,
                unit_t[:].unsqueeze(1).to_broadcast([P, P, PACK]), ALU.mult, ALU.mult,
            )

        def last_product(cols, bank):
            codes, plane = quantise("hid%d" % cols.start, hid[:, cols, :])
            nc.tensor.matmul_mx(
                out=bank[:, cols], lhsT=w3_codes.bitcast(FP8X4), lhsT_scale=w3_plane,
                rhs=codes[:].bitcast(FP8X4), rhs_scale=plane[:], start=True, stop=True,
            )

        def store(cols, bank):
            result = sbuf("result%d" % cols.start, [P, cols.stop - cols.start], F32)
            nc.scalar.copy(result[:], bank[:, cols])
            nc.sync.dma_start(out=out[:, cols], in_=result[:])

        project(0, quantise_weights("w_0", raws[0], nc.scalar.copy))
        invert(0, slice(0, 1))
        invert(0, slice(1, 2))
        project(1, quantise_weights("w_1", raws[1], nc.vector.tensor_copy))
        normalise(0)
        invert(1, slice(0, 2))
        fetch(0, WHOLE, on_vector=(SB,))
        late = sbuf("late_bf16", [P, 2, 2, P, PACK], BF16)
        for n, raw in enumerate(rest):
            nc.vector.tensor_copy(
                out=late[:, :, n].rearrange("p t (c i) s -> p t c s i", i=RUN),
                in_=raw[:].rearrange("p s (t c i) -> p t c s i", t=2, i=RUN),
            )
        late_weights = []
        for n in range(2):
            codes, plane = quantise("late%d" % n, late[:, n].rearrange("p m c s -> p (m c) s"))
            late_weights.append([(codes[:, span], plane[:, span]) for span in (slice(0, P), slice(P, 2 * P))])
        project(2, late_weights[0])
        ((w3_codes, w3_plane),) = quantise_weights("w3", [w3_raw[:]], nc.vector.tensor_copy)
        normalise(1)
        for t in range(TILES - 2):
            multiply(t, WHOLE)
            invert(t + 2, slice(0, 2))
            fetch(t + 1, WHOLE)
            combine(t, WHOLE)
            if t == 0:
                project(LAST, late_weights[1])
            normalise(t + 2)
        for cols in HALVES:
            fetch(LAST, cols)
        multiply(LAST - 1, WHOLE)
        combine(LAST - 1, WHOLE)
        multiply(LAST, HALVES[0])
        combine(LAST, HALVES[0])
        for t in range(LAST):
            exponentiate(t, WHOLE)
        multiply(LAST, HALVES[1])
        combine(LAST, HALVES[1])
        for cols in HALVES:
            exponentiate(LAST, cols)
            for t in range(TILES):
                weigh(t, cols)
        back_banks = [banks[n] for n in (3, 5, 7, 6)]
        for b in range(BLOCKS):
            turn_back(b, back_banks[b])
        for b in range(BLOCKS):
            round_hid(b, back_banks[b])
        last_product(HALVES[0], banks[0])
        store(HALVES[0], banks[0])
        for b in range(HALF // P, BLOCKS):
            last_product(slice(b * P, (b + 1) * P), banks[2])
        store(HALVES[1], banks[2])
